import numpy as np
import ml_dtypes


def mxq(x, axis, fmt="e4m3"):
    dtype, down = {"e4m3": (ml_dtypes.float8_e4m3fn, 7), "e5m2": (ml_dtypes.float8_e5m2, 14)}[fmt]
    v = np.moveaxis(np.asarray(x, np.float32).astype(ml_dtypes.bfloat16).astype(np.float64), axis, -1)
    blocks = v.reshape(v.shape[:-1] + (-1, 32))
    amax = np.abs(blocks).max(-1, keepdims=True)
    byte = np.maximum(np.where(amax > 0, np.frexp(amax)[1] - 1 + 127, 0) - down, 1)
    scale = np.exp2(byte - 127.0)
    codes = (blocks / scale).astype(np.float32).astype(dtype).astype(np.float64)
    return np.moveaxis((codes * scale).reshape(v.shape), -1, axis)


WIDE = False


def mx_kscale(k):
    if not WIDE:
        return np.ones(k)
    levels = np.array([10, -10, 5, -5, 0])
    if k % 512:
        return np.exp2(np.random.permutation(np.resize(levels, k // 32))).repeat(32)
    a = np.empty((k // 512, 16))
    for p in range(k // 512):
        a[p, :8] = np.random.permutation(np.resize(levels, 8))
        for g in range(8):
            far = levels[np.abs(levels - a[p, g]) >= 10]
            a[p, g + 8] = far[np.random.randint(len(far))]
    return np.exp2(a.ravel()).repeat(32)


def f64(x):
    return np.asarray(x).astype(np.float64)


def striped(idx):
    return np.tile(np.asarray(idx).reshape(-1, 16).T, (8, 1)).astype(np.uint16)


def unstriped(offs):
    return offs[:16].T.reshape(-1).astype(np.int64)


E2M1 = np.array([0.0, 0.5, 1.0, 1.5, 2.0, 3.0, 4.0, 6.0, -0.0, -0.5, -1.0, -1.5, -2.0, -3.0, -4.0, -6.0])


def pack_weight(w, fmt):
    k, n = w.shape
    w = f64(np.asarray(w, np.float32).astype(ml_dtypes.bfloat16)).reshape(k // 32, 32, n)
    amax = np.abs(w).max(1)
    if fmt == "e4m3":
        byte = np.frexp(amax)[1] - 1 + 127 - 7
    else:
        mant, ex = np.frexp(amax / 6.0)
        byte = np.where(mant > 0.5, ex, ex - 1) + 127
    byte = np.clip(np.where(amax > 0, byte, 1), 1, 254)
    scaled = (w * np.exp2(127.0 - byte)[:, None, :]).reshape(k, n).astype(np.float32)
    by_word = np.ascontiguousarray(scaled.reshape(k // 512, 128, 4, n).transpose(0, 1, 3, 2))
    if fmt == "e4m3":
        words = by_word.astype(ml_dtypes.float8_e4m3fn).view(np.uint8)
    else:
        c = by_word.astype(ml_dtypes.float4_e2m1fn).view(np.uint8) & 0xF
        words = (c[..., 0::2] | (c[..., 1::2] << 4)).reshape(k // 512, 128, 2 * n)
    return np.ascontiguousarray(words), np.ascontiguousarray(byte.astype(np.uint8).reshape(k // 512, 16, n))


def unpack_weight(words, scales, fmt):
    g, _, n = scales.shape
    words = np.ascontiguousarray(words).reshape(g, 128, n, -1)
    if fmt == "e4m3":
        vals = words.view(ml_dtypes.float8_e4m3fn).astype(np.float64)
    else:
        nib = np.empty((g, 128, n, 4), np.uint8)
        nib[..., 0::2] = words & 0xF
        nib[..., 1::2] = words >> 4
        vals = E2M1[nib]
    vals = vals * np.repeat(np.exp2(scales.astype(np.float64) - 127.0), 8, axis=1)[..., None]
    return vals.transpose(0, 1, 3, 2).reshape(g * 512, n)


def bf(x):
    return np.asarray(x, np.float32).astype(ml_dtypes.bfloat16)


def planes(Y):
    r, m = Y.shape
    b = f64(bf(Y)).reshape(r // 32, 32, m)
    amax = np.abs(b).max(1)
    byte = np.clip(np.where(amax > 0, np.frexp(amax)[1] - 1 + 127 - 7, 1), 1, 254)
    codes = (b * np.exp2(127.0 - byte)[:, None, :]).reshape(r, m).astype(np.float32).astype(ml_dtypes.float8_e4m3fn).view(np.uint8)
    words = codes.reshape(r // 512, 128, 4, m).transpose(0, 1, 3, 2)
    return np.ascontiguousarray(words), np.ascontiguousarray(byte.astype(np.uint8).reshape(r // 512, 16, m))


D, T, I, Q, E, Z, M, C = 512, 2048, 512, 256, 512, 1024, 1024, 512


def setup_inputs():
    n = np.random.standard_normal
    idx = np.random.permutation(T)[:I]
    idx2 = np.random.permutation(Z)[:I]
    idx3 = np.random.permutation(M)[:Q]
    fd = mx_kscale(D)
    fi = mx_kscale(I)
    fc = mx_kscale(C)
    ti = np.ones(T)
    ti[idx] = fi
    keysp = pack_weight(n((D, T)) / fd[:, None], "e2m1")
    return {
        "query": (n((D, Q)) * 1.0 / np.sqrt(D) * fd[:, None]).astype(np.float32),
        "query2": (n((D, Q)) * 1.0 / np.sqrt(D) * fd[:, None]).astype(np.float32),
        "keys_words": keysp[0],
        "keys_scales": keysp[1],
        "pages": (n((D, Z)) / fd[:, None]).astype(np.float32),
        "os": (np.random.uniform(0.02, 0.08, (1, I)) * fi).astype(np.float32),
        "vals": (n((E, T)) / ti).astype(np.float32),
        "wm": (n((C, E)) * 1.0 / np.sqrt(C) * fc[:, None]).astype(np.float32),
        "mstore": (n((C, M)) / fc[:, None]).astype(np.float32),
        "offs": striped(idx),
        "offs2": striped(idx2),
        "offs3": striped(idx3),
    }


def reference(query, query2, keys_words, keys_scales, pages, os, vals, wm, mstore, offs, offs2, offs3):
    idx = unstriped(offs)
    idx2 = unstriped(offs2)
    idx3 = unstriped(offs3)
    keysu = unpack_weight(keys_words, keys_scales, "e2m1")
    queryq = mxq(f64(query), 0, "e4m3")
    keysidxg = keysu[:, idx]
    a = queryq.T @ keysidxg
    query2q = mxq(f64(query2), 0, "e4m3")
    pagesq = mxq(f64(pages), 0, "e4m3")
    h0 = query2q.T @ pagesq
    s = np.maximum(a, h0[:, idx2])
    w = np.maximum(s, 0.0)
    wo1 = w * f64(os)
    wt1 = wo1.T
    vt1 = f64(vals)[:, idx].T
    vt1q = mxq(vt1, 0, "e4m3")
    wt1q = mxq(wt1, 0, "e4m3")
    wmq = mxq(f64(wm), 0, "e4m3")
    mstoreidx3q = mxq(f64(mstore)[:, idx3], 0, "e4m3")
    o = vt1q.T @ wt1q + wmq.T @ mstoreidx3q
    words, scales = planes(o)
    return o, words, scales

from contextlib import ExitStack

import concourse.mybir as mybir
from concourse.masks import make_identity

D, T, I, Q, E, Z, M, C = 512, 2048, 512, 256, 512, 1024, 1024, 512
FLOPS = 2 * (D * Q * I + D * Q * Z + I * E * Q + C * E * Q)

F32 = mybir.dt.float32
BF16 = mybir.dt.bfloat16
I32 = mybir.dt.int32
U32 = mybir.dt.uint32
U16 = mybir.dt.uint16
U8 = mybir.dt.uint8
FP8X4 = mybir.dt.float8_e4m3fn_x4
FP4X4 = mybir.dt.float4_e2m1fn_x4
ALU = mybir.AluOpType
COPY = mybir.ActivationFunctionType.Copy

P = 128
PACK = 4
BANK = 512
HALVES = Q // P
WM_PARTS = 2
WM_COLS = E // WM_PARTS
WM_M = WM_COLS // PACK
PAGES_V = 336
UNIT = 128


def interleave(copy, grouped, raw):
    copy(
        grouped.rearrange("p (c i) j -> p c j i", i=PACK),
        raw.rearrange("p j (c i) -> p c j i", i=PACK),
    )


def tile_attend_widelarger_addedmemory_lean_pl_kernel(
    tc, query, query2, keys_words, keys_scales, pages, factors, vals, wm, mstore, offs, offs2, offs3, out_0, out_1, out_2
):
    nc = tc.nc
    with ExitStack() as ctx:
        sb = ctx.enter_context(tc.tile_pool(name="sb", bufs=1))
        ps = ctx.enter_context(tc.psum_pool(name="ps", bufs=1))

        def mx_operand(name, width):
            codes = sb.tile([P, width], U32, name=name + "_codes", align_bytes=64)
            scales = sb.tile([P, width], U8, name=name + "_scales", align_bytes=64)
            return codes, scales

        def quantize(operand, first, grouped):
            codes, scales = operand
            cols = slice(first, first + grouped.shape[1] // PACK)
            nc.vector.quantize_mx(codes[:, cols].bitcast(FP8X4), scales[:, cols], grouped)

        def rows_by_word(x):
            return x.rearrange("(p j) w -> p j w", j=PACK)

        def by_word(flat):
            return flat.rearrange("p (w j) -> p w j", j=PACK)

        def scalar_copy(dst, src):
            nc.scalar.activation(dst, src, COPY)

        key_scales = sb.tile([P, T], U8)
        nc.gpsimd.memset(key_scales[:].bitcast(I32), 0)
        identity = sb.tile([P, P], F32)
        make_identity(nc, identity[:])
        for quad in range(4):
            nc.scalar.dma_start(
                key_scales[32 * quad : 32 * quad + 4, :].bitcast(I32),
                keys_scales[0, 4 * quad : 4 * quad + 4, :].bitcast(I32),
            )
        slot_factor = sb.tile([P, PACK], F32)
        nc.scalar.dma_start(slot_factor[:], factors.rearrange("o (p t) -> p (o t)", t=PACK))

        query2_raw = sb.tile([P, PACK, Q], F32)
        nc.sync.dma_start(query2_raw[:], rows_by_word(query2))
        token_list = sb.tile([P, I // 16], U16)
        nc.sync.dma_start(token_list[:], offs)
        pages_raw = [
            sb.tile([P, PACK, BANK], F32, name="pages_raw%d" % n, tag="pages%d" % n, align_bytes=64)
            for n in range(Z // BANK)
        ]
        for n in range(Z // BANK):
            nc.sync.dma_start(pages_raw[n][:], rows_by_word(pages)[:, :, n * BANK : (n + 1) * BANK])
        query_raw = sb.tile([P, PACK, Q], F32)
        nc.sync.dma_start(query_raw[:], rows_by_word(query))
        key_words = sb.tile([P, T], U16)
        nc.sync.dma_start(key_words[:].bitcast(I32), keys_words[0].bitcast(I32))
        page_list = sb.tile([P, I // 16], U16)
        nc.sync.dma_start(page_list[:], offs2)
        column_list = sb.tile([P, Q // 16], U16)
        nc.sync.dma_start(column_list[:], offs3)
        mstore_raw = [sb.tile([P, M], F32, name="mstore_raw%d" % j) for j in range(PACK)]
        for j in range(PACK):
            nc.sync.dma_start(mstore_raw[j][:], rows_by_word(mstore)[:, j, :])
        vals_raw = [sb.tile([P, T], F32, name="vals_raw%d" % r) for r in range(PACK)]
        wm_raw = [sb.tile([P, PACK, WM_COLS], F32, name="wm_raw%d" % n) for n in range(WM_PARTS)]
        for r in range(PACK):
            nc.sync.dma_start(vals_raw[r][:], rows_by_word(vals)[:, r, :])
            if r >= PACK - WM_PARTS:
                n = r - (PACK - WM_PARTS)
                nc.sync.dma_start(wm_raw[n][:], rows_by_word(wm)[:, :, n * WM_COLS : (n + 1) * WM_COLS])

        queries_bf = sb.tile([P, 2 * Q * PACK], BF16, align_bytes=64)
        queries_mx = mx_operand("queries", 2 * Q)
        interleave(nc.vector.tensor_copy, by_word(queries_bf[:, 0 : Q * PACK]), query2_raw[:])
        quantize(queries_mx, 0, queries_bf[:, 0 : Q * PACK])

        h0 = [sb.tile([P, Z], F32, name="h0_%d" % h) for h in range(HALVES)]
        for n in range(Z // BANK):
            pages_bf = sb.tile([P, BANK * PACK], BF16, name="pages_bf%d" % n, align_bytes=64)
            split = BANK if n == 0 else PAGES_V
            interleave(nc.vector.tensor_copy, by_word(pages_bf[:])[:, 0:split, :], pages_raw[n][:, :, 0:split])
            if split < BANK:
                interleave(nc.scalar.copy, by_word(pages_bf[:])[:, split:BANK, :], pages_raw[n][:, :, split:BANK])
            pages_mx = mx_operand("pages%d" % n, BANK)
            quantize(pages_mx, 0, pages_bf[:])
            for h in range(HALVES):
                rows = slice(h * P, (h + 1) * P)
                bank = ps.tile([P, BANK], F32, name="score", tag="score", bufs=4)
                nc.tensor.matmul_mx(
                    bank[:], queries_mx[0][:, rows].bitcast(FP8X4), queries_mx[1][:, rows],
                    pages_mx[0][:].bitcast(FP8X4), pages_mx[1][:], start=True, stop=True,
                )
                nc.scalar.copy(h0[h][:, n * BANK : (n + 1) * BANK], bank[:])

        listed_scales = sb.tile([P, I], U8, tag="pages0", align_bytes=64)
        nc.vector.tensor_copy(listed_scales[:], key_scales[:].indirect(token_list[:]))
        interleave(nc.vector.tensor_copy, by_word(queries_bf[:, Q * PACK : 2 * Q * PACK]), query_raw[:])
        listed_words = sb.tile([P, I], U16, tag="pages1", align_bytes=64)
        nc.vector.tensor_copy(listed_words[:], key_words[:].indirect(token_list[:]))
        quantize(queries_mx, Q, queries_bf[:, Q * PACK : 2 * Q * PACK])
        positive = [sb.tile([P, I], F32, name="positive%d" % h, align_bytes=64) for h in range(HALVES)]
        early = sb.tile([P, I], F32, align_bytes=64)
        late = sb.tile([P, 11 * UNIT], F32, align_bytes=64)

        def units(first, count):
            return late[:, first * UNIT : (first + count) * UNIT]

        weights_bf = units(7, 4).bitcast(BF16)

        for h in range(HALVES):
            rows = slice(Q + h * P, Q + (h + 1) * P)
            listed_h0 = early[:] if h == 0 else units(3, 4)
            (nc.vector.tensor_copy, scalar_copy)[h](listed_h0, h0[h][:].indirect(page_list[:]))
            bank = ps.tile([P, BANK], F32, name="score", tag="score", bufs=4)
            nc.tensor.matmul_mx(
                bank[:], queries_mx[0][:, rows].bitcast(FP8X4), queries_mx[1][:, rows],
                listed_words[:].bitcast(FP4X4), listed_scales[:], start=True, stop=True,
            )
            nc.vector.scalar_tensor_tensor(
                positive[h][:].rearrange("p (t s) -> p s t", t=PACK),
                bank[:].rearrange("p (s t) -> p s t", t=PACK),
                0.0,
                listed_h0.rearrange("p (s t) -> p s t", t=PACK),
                ALU.max,
                ALU.max,
            )
            turned = ps.tile([P, PACK, P], F32, name="turned", tag="turned", bufs=2)
            for t in range(PACK):
                nc.tensor.transpose(turned[:, t, :], positive[h][:, t * P : (t + 1) * P], identity[:])
            nc.vector.tensor_tensor(
                by_word(weights_bf)[:, h * P : (h + 1) * P, :],
                turned[:].rearrange("p t q -> p q t"),
                slot_factor[:].unsqueeze(1).to_broadcast([P, P, PACK]),
                ALU.mult,
            )
        weights_mx = mx_operand("weights", Q)
        quantize(weights_mx, 0, weights_bf)

        listed_store = early[:].bitcast(BF16).rearrange("p (j q) -> p j q", j=PACK)
        for j in range(PACK):
            (scalar_copy, nc.vector.tensor_copy)[j // 2](listed_store[:, j, :], mstore_raw[j][:].indirect(column_list[:]))
        memory_bf = units(3, 4).bitcast(BF16)
        interleave(nc.vector.tensor_copy, by_word(memory_bf), listed_store)
        memory_mx = mx_operand("memory", Q)
        quantize(memory_mx, 0, memory_bf)

        sums = [ps.tile([P, PACK, P], F32, name="sums%d" % h) for h in range(HALVES)]
        wm_mx = mx_operand("wm", E)

        def quantize_wm(n):
            wm_bf = units(3 if n == 0 else 0, 4).bitcast(BF16)
            nc.vector.tensor_copy(
                wm_bf.rearrange("p (r m j) -> p m j r", r=PACK, j=PACK),
                wm_raw[n][:].rearrange("p j (m r) -> p m j r", r=PACK),
            )
            for r in (reversed(range(PACK)) if n == 0 else range(PACK)):
                quantize(wm_mx, r * P + n * WM_M, wm_bf[:, r * WM_M * PACK : (r + 1) * WM_M * PACK])

        for r in range(PACK):
            if r == PACK - 1:
                quantize_wm(0)
            pairs = (positive[0][:, 0 : I // 2], positive[1][:, 0 : I // 2], units(7, 2), units(6, 2))[r]
            listed_vals = pairs.bitcast(BF16)
            if r < PACK - 2:
                nc.scalar.activation(listed_vals, vals_raw[r][:].indirect(token_list[:]), COPY)
            else:
                nc.vector.tensor_copy(listed_vals[:, 0 : I // 2], vals_raw[r][:].indirect(token_list[:, 0 : I // 32]))
                nc.scalar.activation(
                    listed_vals[:, I // 2 : I], vals_raw[r][:].indirect(token_list[:, I // 32 : I // 16]), COPY
                )
            turned = ps.tile([P, PACK, P], F32, name="turned", tag="turned", bufs=2)
            for u in range(2):
                nc.tensor.transpose(turned[:, u, :], pairs[:, u : I // 2 : 2], identity[:])
            values_bf = sb.tile([P, P * PACK], BF16, name="values_bf%d" % r, align_bytes=64)[:]
            nc.scalar.copy(
                values_bf.bitcast(F32).rearrange("p (e u) -> p e u", u=2),
                turned[:, 0:2, :].rearrange("p u e -> p e u"),
            )
            values_mx = mx_operand("values%d" % r, P)
            quantize(values_mx, 0, values_bf)
            for h in range(HALVES):
                cols = slice(h * P, (h + 1) * P)
                nc.tensor.matmul_mx(
                    sums[h][:, r, :], values_mx[0][:].bitcast(FP8X4), values_mx[1][:],
                    weights_mx[0][:, cols].bitcast(FP8X4), weights_mx[1][:, cols], start=(r == 0), stop=False,
                )

        quantize_wm(1)
        for r in range(PACK):
            feats = slice(r * P, (r + 1) * P)
            for h in range(HALVES):
                cols = slice(h * P, (h + 1) * P)
                nc.tensor.matmul_mx(
                    sums[h][:, r, :], wm_mx[0][:, feats].bitcast(FP8X4), wm_mx[1][:, feats],
                    memory_mx[0][:, cols].bitcast(FP8X4), memory_mx[1][:, cols], start=False, stop=(r == PACK - 1),
                )

        result = sb.tile([P, PACK, Q], F32)
        result_bf = sb.tile([P, Q, PACK], BF16, align_bytes=64)
        copies = (nc.vector.tensor_copy, nc.scalar.copy)
        for h in range(HALVES):
            copies[h](result[:, :, h * P : (h + 1) * P], sums[h][:])
        nc.sync.dma_start(rows_by_word(out_0), result[:])
        for h in range(HALVES):
            copies[h](result_bf[:, h * P : (h + 1) * P, :], sums[h][:].rearrange("p r q -> p q r"))
        result_mx = mx_operand("result", Q)
        quantize(result_mx, 0, result_bf[:].rearrange("p w j -> p (w j)"))
        nc.sync.dma_start(out_1[0].rearrange("p c r -> p (c r)").bitcast(I32), result_mx[0][:].bitcast(I32))
        for quad in range(4):
            queue = nc.scalar if quad % 2 == 0 else nc.sync
            queue.dma_start(
                out_2[0, 4 * quad : 4 * quad + 4, :].bitcast(I32),
                result_mx[1][32 * quad : 32 * quad + 4, :].bitcast(I32),
            )
